import numpy as np
CORES = [0,7,8,15,16,23,24,31,32,39,40,47,48,55,56,63]
N = 16
def setup_inputs(rng):
    return {"x": rng.standard_normal((N, 128, 1024), dtype=np.float32)}
def reference(x):
    s = np.cumsum(x.astype(np.float64), axis=0)
    y = np.full(x.shape, np.nan, x.dtype)
    y[1:] = s[:-1]
    return {"y": y}

from concourse.bass import DstId, RemoteDMATransfer

NCH = 4
NT = 2 * NCH
ROWS = 128 // NT
W = ROWS * 1024 // 128
HELPER = (6, 3)

LO, HI = 0x00FF, 0xFF00
HI_A, HI_B = 0x0F00, 0xF000

SCRATCH = {
    "xs": ("dram", [NT, 128, W], "float32"),
    "yl": ("dram", [NT, 128, W], "float32"),
    "xa": ("dram", [NCH, 128, W], "float32"),
    "xb": ("dram", [NCH, 128, W], "float32"),
    "cm": ("dram", [NCH, 128, W], "float32"),
    "q": ("dram", [NCH, 128, W], "float32"),
}
SEMAPHORES = ["sent", "st"] + ["%s%d" % (n, j) for n in ("ld", "y", "xin", "cm", "q") for j in range(NCH)]


def rank_program(g, core, T, topo):
    chip, k = topo.chip(core), core % 8
    m, odd = chip // 2, chip % 2
    first, second = chip * 8, chip * 8 + 7

    def did(c):
        rid, pid, _se = topo.addr(c)
        return DstId(rid=rid, pnc=pid)

    def move(dst_core, mask, sem, srcs, dst):
        return RemoteDMATransfer(dst_ids=[did(dst_core)], dma_engine_mask=mask, remote_sem=sem,
                                 srcs=srcs, dsts=[dst], alu_op=1 if len(srcs) > 1 else 0)

    def engines(transfers_masks):
        return sum(bin(x).count("1") for x in transfers_masks)

    if k in (0, 7):
        queues = (g.sync, g.scalar)
        sent = stored = 0
        if core != T.cores[-1]:
            for j in range(NCH):
                queues[j % 2].dma_start(T.xs[2 * j:2 * j + 2], T.x[2 * j * ROWS:(2 * j + 2) * ROWS, :]) \
                    .then_inc(T.sem["ld%d" % j], 16)
            land = T.xa if k == 0 else T.xb
            for j in range(NCH):
                g.wait_ge(T.sem["ld%d" % j], 16)
                g.remote_dma_fused([move(first + HELPER[h], (LO, HI)[h], T.sem["xin%d" % j], [T.xs[2 * j + h]], land[j])
                                    for h in range(2)], local_sem=T.sem.sent)
                sent += 16
        if core != T.cores[0]:
            per_helper = 4 if 0 < chip < 6 else 8
            for j in range(NCH):
                queues[j % 2].wait_ge(T.sem["y%d" % j], 2 * per_helper)
                queues[j % 2].dma_start(T.y[2 * j * ROWS:(2 * j + 2) * ROWS, :], T.yl[2 * j:2 * j + 2]) \
                    .then_inc(T.sem.st, 16)
                stored += 16
        if sent:
            g.wait_ge(T.sem.sent, sent)
        if stored:
            g.wait_ge(T.sem.st, stored)
        return

    if k not in HELPER:
        return
    h = HELPER.index(k)
    sent = 0

    for j in range(NCH):
        g.wait_ge(T.sem["xin%d" % j], 8 if chip == 7 else 16)
        tr, masks = [], []
        if chip != 7:
            tr.append(move(core ^ 8, LO, T.sem["cm%d" % j], [T.xa[j], T.xb[j]], T.cm[j]))
            masks.append(LO)
        if chip == 0:
            tr.append(move(second, HI, T.sem["y%d" % j], [T.xa[j]], T.yl[2 * j + h]))
            masks.append(HI)
        if tr:
            g.remote_dma_fused(tr, local_sem=T.sem.sent)
            sent += engines(masks)

    for j in range(NCH):
        if chip != 6:
            g.wait_ge(T.sem["cm%d" % j], 8)
        if m > 0:
            g.wait_ge(T.sem["q%d" % j], 8)
        before_pair = [T.q[j]] if m > 0 else []
        before_chip = before_pair + ([T.cm[j]] if odd else [])
        tr, masks = [], []
        if m < 3:
            tr.append(move(core + 16, LO, T.sem["q%d" % j], before_pair + [T.cm[j], T.xa[j], T.xb[j]], T.q[j]))
            masks.append(LO)
        if chip > 0:
            ma, mb = (HI_A, HI_B) if m < 3 else (LO, HI)
            tr.append(move(first, ma, T.sem["y%d" % j], before_chip, T.yl[2 * j + h]))
            tr.append(move(second, mb, T.sem["y%d" % j], before_chip + [T.xa[j]], T.yl[2 * j + h]))
            masks += [ma, mb]
        g.remote_dma_fused(tr, local_sem=T.sem.sent)
        sent += engines(masks)
    g.wait_ge(T.sem.sent, sent)
